import numpy as np
import ml_dtypes

BF16 = ml_dtypes.bfloat16


def bf(x):
    return np.asarray(x, np.float32).astype(BF16)


def f32(x):
    return np.asarray(x, np.float32)


def f64(x):
    return np.asarray(x).astype(np.float64)


def striped(idx):
    return np.tile(idx.reshape(-1, 16).T, (8, 1))


S, K, M, N = 4096, 256, 128, 4096


def setup_inputs():
    return {"table": bf(np.random.standard_normal((K, S))), "w": bf(np.random.standard_normal((K, M)) / np.sqrt(K)), "s": f32(0.5 + np.random.random_sample((M, 1))), "b": f32(0.5 * np.random.standard_normal((M, 1))), "offs": striped(np.random.permutation(np.tile(np.arange(S), 2))[:N])}


def reference(table, w, s, b, offs):
    idx = offs[:16].T.reshape(-1)
    x = f64(table)[:, idx]
    y = f64(w).T @ x
    return y * f64(s) + f64(b)

@@ -1,0 +1,54 @@
+import concourse.mybir as mybir
+
+BF16, F32, U16 = mybir.dt.bfloat16, mybir.dt.float32, mybir.dt.uint16
+MULT, ADD = mybir.AluOpType.mult, mybir.AluOpType.add
+IDENTITY = mybir.ActivationFunctionType.Identity
+
+P = 128
+K, S = 256, 4096
+M, N = 128, 4096
+BLOCKS = K // P
+PIECE = 512
+PIECES = N // PIECE
+COLS = PIECE // 16
+
+FLOPS = 2 * K * M * N
+
+
+def tile_gather_matmul_kernel(tc, table, w, s, b, offs, out):
+    nc = tc.nc
+    with (
+        tc.tile_pool(name="held", bufs=1) as held,
+        tc.psum_pool(name="psum", bufs=1) as psum,
+    ):
+        offsets = held.tile([P, N // 16], U16, name="offsets")
+        nc.sync.dma_start(offsets[:], offs)
+        windows = []
+        for k in range(BLOCKS):
+            window = held.tile([P, S], BF16, name=f"window{k}")
+            nc.sync.dma_start(window[:], table[k * P : (k + 1) * P, :])
+            windows.append(window)
+        weights = held.tile([P, BLOCKS, M], BF16, name="weights")
+        nc.scalar.dma_start(weights[:], w.rearrange("(k p) m -> p k m", p=P))
+        gain = held.tile([P, 1], F32, name="gain")
+        nc.scalar.dma_start(gain[:], s)
+        shift = held.tile([P, 1], F32, name="shift")
+        nc.scalar.dma_start(shift[:], b)
+
+        banks = [psum.tile([P, PIECE], F32, name=f"bank{j}") for j in range(PIECES)]
+        staged = held.tile([P, N], F32, name="staged")
+
+        for k in range(BLOCKS):
+            for j in range(PIECES):
+                picked = windows[k][:].indirect(offsets[:, j * COLS : (j + 1) * COLS])
+                nc.tensor.matmul(
+                    banks[j][:], weights[:, k, :], picked, start=(k == 0), stop=(k == BLOCKS - 1)
+                )
+
+        for j in range(PIECES):
+            piece = staged[:, j * PIECE : (j + 1) * PIECE]
+            if j % 2 == 0:
+                nc.scalar.activation(piece, banks[j][:], IDENTITY, bias=shift[:], scale=gain[:])
+            else:
+                nc.vector.tensor_scalar(piece, banks[j][:], gain[:], shift[:], MULT, ADD)
+            nc.sync.dma_start(out[:, j * PIECE : (j + 1) * PIECE], piece)

@@ -11,6 +11,7 @@ BLOCKS = K // P
 PIECE = 512
 PIECES = N // PIECE
 COLS = PIECE // 16
+WARM = 8
 
 FLOPS = 2 * K * M * N
 
@@ -37,6 +38,11 @@ def tile_gather_matmul_kernel(tc, table, w, s, b, offs, out):
 
         banks = [psum.tile([P, PIECE], F32, name=f"bank{j}") for j in range(PIECES)]
         staged = held.tile([P, N], F32, name="staged")
+
+        zeros = held.tile([P, PIECE], BF16, name="zeros")
+        nc.vector.memset(zeros[:], 0.0)
+        for i in range(WARM):
+            nc.tensor.matmul(banks[PIECES - 1][:], zeros[:, 0:M], zeros[:], start=True, stop=True)
 
         for k in range(BLOCKS):
             for j in range(PIECES):

@@ -11,7 +11,7 @@ BLOCKS = K // P
 PIECE = 512
 PIECES = N // PIECE
 COLS = PIECE // 16
-WARM = 8
+HEAD = 5
 
 FLOPS = 2 * K * M * N
 
@@ -39,22 +39,26 @@ def tile_gather_matmul_kernel(tc, table, w, s, b, offs, out):
         banks = [psum.tile([P, PIECE], F32, name=f"bank{j}") for j in range(PIECES)]
         staged = held.tile([P, N], F32, name="staged")
 
-        zeros = held.tile([P, PIECE], BF16, name="zeros")
-        nc.vector.memset(zeros[:], 0.0)
-        for i in range(WARM):
-            nc.tensor.matmul(banks[PIECES - 1][:], zeros[:, 0:M], zeros[:], start=True, stop=True)
+        def product(k, j):
+            picked = windows[k][:].indirect(offsets[:, j * COLS : (j + 1) * COLS])
+            nc.tensor.matmul(
+                banks[j][:], weights[:, k, :], picked, start=(k == 0), stop=(k == BLOCKS - 1)
+            )
 
-        for k in range(BLOCKS):
-            for j in range(PIECES):
-                picked = windows[k][:].indirect(offsets[:, j * COLS : (j + 1) * COLS])
-                nc.tensor.matmul(
-                    banks[j][:], weights[:, k, :], picked, start=(k == 0), stop=(k == BLOCKS - 1)
-                )
-
-        for j in range(PIECES):
+        def finish(j):
             piece = staged[:, j * PIECE : (j + 1) * PIECE]
             if j % 2 == 0:
                 nc.scalar.activation(piece, banks[j][:], IDENTITY, bias=shift[:], scale=gain[:])
             else:
                 nc.vector.tensor_scalar(piece, banks[j][:], gain[:], shift[:], MULT, ADD)
             nc.sync.dma_start(out[:, j * PIECE : (j + 1) * PIECE], piece)
+
+        for j in range(HEAD):
+            product(0, j)
+        for j in range(HEAD):
+            product(1, j)
+            finish(j)
+        for j in range(HEAD, PIECES):
+            product(0, j)
+            product(1, j)
+            finish(j)

@@ -11,7 +11,7 @@ BLOCKS = K // P
 PIECE = 512
 PIECES = N // PIECE
 COLS = PIECE // 16
-HEAD = 5
+RING = 5
 
 FLOPS = 2 * K * M * N
 
@@ -20,45 +20,34 @@ def tile_gather_matmul_kernel(tc, table, w, s, b, offs, out):
     nc = tc.nc
     with (
         tc.tile_pool(name="held", bufs=1) as held,
-        tc.psum_pool(name="psum", bufs=1) as psum,
+        tc.psum_pool(name="psum", bufs=RING) as psum,
     ):
         offsets = held.tile([P, N // 16], U16, name="offsets")
         nc.sync.dma_start(offsets[:], offs)
+        weights = held.tile([P, BLOCKS, M], BF16, name="weights")
+        nc.scalar.dma_start(weights[:], w.rearrange("(k p) m -> p k m", p=P))
         windows = []
         for k in range(BLOCKS):
             window = held.tile([P, S], BF16, name=f"window{k}")
             nc.sync.dma_start(window[:], table[k * P : (k + 1) * P, :])
             windows.append(window)
-        weights = held.tile([P, BLOCKS, M], BF16, name="weights")
-        nc.scalar.dma_start(weights[:], w.rearrange("(k p) m -> p k m", p=P))
         gain = held.tile([P, 1], F32, name="gain")
-        nc.scalar.dma_start(gain[:], s)
+        nc.sync.dma_start(gain[:], s)
         shift = held.tile([P, 1], F32, name="shift")
-        nc.scalar.dma_start(shift[:], b)
+        nc.sync.dma_start(shift[:], b)
 
-        banks = [psum.tile([P, PIECE], F32, name=f"bank{j}") for j in range(PIECES)]
         staged = held.tile([P, N], F32, name="staged")
 
-        def product(k, j):
-            picked = windows[k][:].indirect(offsets[:, j * COLS : (j + 1) * COLS])
-            nc.tensor.matmul(
-                banks[j][:], weights[:, k, :], picked, start=(k == 0), stop=(k == BLOCKS - 1)
-            )
-
-        def finish(j):
+        for j in range(PIECES):
+            bank = psum.tile([P, PIECE], F32, name="bank")
+            for k in range(BLOCKS):
+                picked = windows[k][:].indirect(offsets[:, j * COLS : (j + 1) * COLS])
+                nc.tensor.matmul(
+                    bank[:], weights[:, k, :], picked, start=(k == 0), stop=(k == BLOCKS - 1)
+                )
             piece = staged[:, j * PIECE : (j + 1) * PIECE]
             if j % 2 == 0:
-                nc.scalar.activation(piece, banks[j][:], IDENTITY, bias=shift[:], scale=gain[:])
+                nc.scalar.activation(piece, bank[:], IDENTITY, bias=shift[:], scale=gain[:])
             else:
-                nc.vector.tensor_scalar(piece, banks[j][:], gain[:], shift[:], MULT, ADD)
+                nc.vector.tensor_scalar(piece, bank[:], gain[:], shift[:], MULT, ADD)
             nc.sync.dma_start(out[:, j * PIECE : (j + 1) * PIECE], piece)
-
-        for j in range(HEAD):
-            product(0, j)
-        for j in range(HEAD):
-            product(1, j)
-            finish(j)
-        for j in range(HEAD, PIECES):
-            product(0, j)
-            product(1, j)
-            finish(j)

@@ -32,9 +32,9 @@ def tile_gather_matmul_kernel(tc, table, w, s, b, offs, out):
             nc.sync.dma_start(window[:], table[k * P : (k + 1) * P, :])
             windows.append(window)
         gain = held.tile([P, 1], F32, name="gain")
-        nc.sync.dma_start(gain[:], s)
+        nc.scalar.dma_start(gain[:], s)
         shift = held.tile([P, 1], F32, name="shift")
-        nc.sync.dma_start(shift[:], b)
+        nc.scalar.dma_start(shift[:], b)
 
         staged = held.tile([P, N], F32, name="staged")
 

@@ -11,7 +11,7 @@ BLOCKS = K // P
 PIECE = 512
 PIECES = N // PIECE
 COLS = PIECE // 16
-RING = 5
+RING = 4
 
 FLOPS = 2 * K * M * N
 

@@ -12,6 +12,7 @@ PIECE = 512
 PIECES = N // PIECE
 COLS = PIECE // 16
 RING = 4
+LAST_PARTS = 2
 
 FLOPS = 2 * K * M * N
 
@@ -45,9 +46,14 @@ def tile_gather_matmul_kernel(tc, table, w, s, b, offs, out):
                 nc.tensor.matmul(
                     bank[:], weights[:, k, :], picked, start=(k == 0), stop=(k == BLOCKS - 1)
                 )
-            piece = staged[:, j * PIECE : (j + 1) * PIECE]
-            if j % 2 == 0:
-                nc.scalar.activation(piece, bank[:], IDENTITY, bias=shift[:], scale=gain[:])
-            else:
-                nc.vector.tensor_scalar(piece, bank[:], gain[:], shift[:], MULT, ADD)
-            nc.sync.dma_start(out[:, j * PIECE : (j + 1) * PIECE], piece)
+            parts = LAST_PARTS if j == PIECES - 1 else 1
+            width = PIECE // parts
+            for h in range(parts):
+                closed = bank[:, h * width : (h + 1) * width]
+                first = j * PIECE + h * width
+                part = staged[:, first : first + width]
+                if j % 2 == 0:
+                    nc.scalar.activation(part, closed, IDENTITY, bias=shift[:], scale=gain[:])
+                else:
+                    nc.vector.tensor_scalar(part, closed, gain[:], shift[:], MULT, ADD)
+                nc.sync.dma_start(out[:, first : first + width], part)

@@ -11,7 +11,7 @@ BLOCKS = K // P
 PIECE = 512
 PIECES = N // PIECE
 COLS = PIECE // 16
-RING = 4
+RING = 5
 LAST_PARTS = 2
 
 FLOPS = 2 * K * M * N

@@ -26,11 +26,12 @@ def tile_gather_matmul_kernel(tc, table, w, s, b, offs, out):
         offsets = held.tile([P, N // 16], U16, name="offsets")
         nc.sync.dma_start(offsets[:], offs)
         weights = held.tile([P, BLOCKS, M], BF16, name="weights")
-        nc.scalar.dma_start(weights[:], w.rearrange("(k p) m -> p k m", p=P))
+        nc.scalar.dma_start(weights[:], w.rearrange("(p k) m -> p k m", k=BLOCKS))
+        features = table.rearrange("(p k) s -> k p s", k=BLOCKS)
         windows = []
         for k in range(BLOCKS):
             window = held.tile([P, S], BF16, name=f"window{k}")
-            nc.sync.dma_start(window[:], table[k * P : (k + 1) * P, :])
+            nc.sync.dma_start(window[:], features[k])
             windows.append(window)
         gain = held.tile([P, 1], F32, name="gain")
         nc.scalar.dma_start(gain[:], s)

import concourse.mybir as mybir

BF16, F32, U16 = mybir.dt.bfloat16, mybir.dt.float32, mybir.dt.uint16
MULT, ADD = mybir.AluOpType.mult, mybir.AluOpType.add
IDENTITY = mybir.ActivationFunctionType.Identity

P = 128
K, S = 256, 4096
M, N = 128, 4096
BLOCKS = K // P
PIECE = 512
PIECES = N // PIECE
COLS = PIECE // 16
RING = 5
LAST_PARTS = 2

FLOPS = 2 * K * M * N


def tile_gather_matmul_kernel(tc, table, w, s, b, offs, out):
    nc = tc.nc
    with (
        tc.tile_pool(name="held", bufs=1) as held,
        tc.psum_pool(name="psum", bufs=RING) as psum,
    ):
        offsets = held.tile([P, N // 16], U16, name="offsets")
        nc.sync.dma_start(offsets[:], offs)
        weights = held.tile([P, BLOCKS, M], BF16, name="weights")
        nc.scalar.dma_start(weights[:], w.rearrange("(p k) m -> p k m", k=BLOCKS))
        features = table.rearrange("(p k) s -> k p s", k=BLOCKS)
        windows = []
        for k in range(BLOCKS):
            window = held.tile([P, S], BF16, name=f"window{k}")
            nc.sync.dma_start(window[:], features[k])
            windows.append(window)
        gain = held.tile([P, 1], F32, name="gain")
        nc.scalar.dma_start(gain[:], s)
        shift = held.tile([P, 1], F32, name="shift")
        nc.scalar.dma_start(shift[:], b)

        staged = held.tile([P, N], F32, name="staged")

        for j in range(PIECES):
            bank = psum.tile([P, PIECE], F32, name="bank")
            for k in range(BLOCKS):
                picked = windows[k][:].indirect(offsets[:, j * COLS : (j + 1) * COLS])
                nc.tensor.matmul(
                    bank[:], weights[:, k, :], picked, start=(k == 0), stop=(k == BLOCKS - 1)
                )
            parts = LAST_PARTS if j == PIECES - 1 else 1
            width = PIECE // parts
            for h in range(parts):
                closed = bank[:, h * width : (h + 1) * width]
                first = j * PIECE + h * width
                part = staged[:, first : first + width]
                if j % 2 == 0:
                    nc.scalar.activation(part, closed, IDENTITY, bias=shift[:], scale=gain[:])
                else:
                    nc.vector.tensor_scalar(part, closed, gain[:], shift[:], MULT, ADD)
                nc.sync.dma_start(out[:, first : first + width], part)
